import numpy as np
import ml_dtypes


def mxq(x, axis, fmt="e4m3"):
    dtype, down = {"e4m3": (ml_dtypes.float8_e4m3fn, 7), "e5m2": (ml_dtypes.float8_e5m2, 14)}[fmt]
    v = np.moveaxis(np.asarray(x, np.float32).astype(ml_dtypes.bfloat16).astype(np.float64), axis, -1)
    blocks = v.reshape(v.shape[:-1] + (-1, 32))
    amax = np.abs(blocks).max(-1, keepdims=True)
    byte = np.maximum(np.where(amax > 0, np.frexp(amax)[1] - 1 + 127, 0) - down, 1)
    scale = np.exp2(byte - 127.0)
    codes = (blocks / scale).astype(np.float32).astype(dtype).astype(np.float64)
    return np.moveaxis((codes * scale).reshape(v.shape), -1, axis)


WIDE = False


def mx_kscale(k):
    if not WIDE:
        return np.ones(k)
    levels = np.array([10, -10, 5, -5, 0])
    if k % 512:
        return np.exp2(np.random.permutation(np.resize(levels, k // 32))).repeat(32)
    a = np.empty((k // 512, 16))
    for p in range(k // 512):
        a[p, :8] = np.random.permutation(np.resize(levels, 8))
        for g in range(8):
            far = levels[np.abs(levels - a[p, g]) >= 10]
            a[p, g + 8] = far[np.random.randint(len(far))]
    return np.exp2(a.ravel()).repeat(32)


def f64(x):
    return np.asarray(x).astype(np.float64)


def striped(idx):
    return np.tile(idx.reshape(-1, 16).T, (8, 1)).astype(np.uint16)


def unstriped(offs):
    return offs[:16].T.reshape(-1).astype(np.int64)


def relu2(v):
    return np.maximum(v, 0.0) ** 2


K, T, E, C, H, N = 1536, 1024, 6, 128, 512, 256


def by_expert(wq, xq):
    return np.concatenate([wq[e].T @ xq[:, e * C:(e + 1) * C] for e in range(E)], axis=1)


def setup_inputs():
    n = np.random.standard_normal
    s = mx_kscale(K)[:, None]
    u = mx_kscale(H)
    return {
        "xT": (n((K, T)) * s).astype(np.float32),
        "w1": (n((E, K, H)) / np.sqrt(K) / s[None] * u[None, None, :]).astype(np.float32),
        "w2": (n((E, H, N)) / np.sqrt(H) / u[None, :, None] ** 2).astype(np.float32),
        "gate": np.tile(np.random.uniform(0.2, 1.0, E * C), (N, 1)).astype(np.float32),
        "offs": striped(np.random.permutation(T)[:E * C]),
        "dst": striped(np.random.permutation(T)[:E * C]),
    }


def reference(xT, w1, w2, gate, offs, dst):
    idx = unstriped(offs)
    xq = mxq(f64(xT)[:, idx], 0, "e4m3")
    h = relu2(by_expert(mxq(f64(w1), 1, "e4m3"), xq))
    y = by_expert(mxq(f64(w2), 1, "e4m3"), mxq(h, 0, "e4m3"))
    out = np.zeros((N, T))
    out[:, unstriped(dst)] = f64(gate) * y
    return out

@@ -1,0 +1,253 @@
+from contextlib import ExitStack
+
+import concourse.mybir as mybir
+
+K, T, E, C, H, N = 1536, 1024, 6, 128, 512, 256
+FLOPS = 2 * E * C * (K * H + H * N)
+
+F32 = mybir.dt.float32
+BF16 = mybir.dt.bfloat16
+U32 = mybir.dt.uint32
+U16 = mybir.dt.uint16
+U8 = mybir.dt.uint8
+FP8X4 = mybir.dt.float8_e4m3fn_x4
+RELU = mybir.ActivationFunctionType.Relu
+SQUARE = mybir.ActivationFunctionType.Square
+MULT = mybir.AluOpType.mult
+
+P = 128
+PACK = 4
+PASS = P * PACK
+PASSES = K // PASS
+CHUNK = 512
+SLOTS = E * C
+LEAD = 9
+LAST = E - 1
+
+
+def tile_moe_two_mlp_relu2_kernel(tc, xT, w1, w2, gate, offs, dst, out):
+    nc = tc.nc
+
+    x_eng = [[('V', 0, 16)], [('V', 0, 16)], [('S', 0, 16)], [('V', 0, 16)], [('S', 0, 16)], [('V', 0, 8), ('S', 8, 16)]]
+    w1_eng = [[[('S', 0, 16)], [('S', 0, 16)], [('S', 0, 16)]], [[('S', 0, 16)], [('V', 0, 16)], [('V', 0, 16)]], [[('S', 0, 16)], [('V', 0, 16)], [('S', 0, 16)]], [[('S', 0, 16)], [('V', 0, 16)], [('S', 0, 16)]], [[('S', 0, 16)], [('V', 0, 16)], [('S', 0, 16)]], [[('S', 0, 16)], [('V', 0, 16)], [('V', 0, 8), ('S', 8, 16)]]]
+    w2_eng = [[('V', 0, 16)], [('V', 0, 16)], [('V', 0, 16)], [('V', 0, 16)], [('V', 0, 16)], [('S', 0, 16)], [('V', 0, 16)]]
+    units = []
+    for i in range(2 * PASSES):
+        units.append(("x", i // 2, i % 2 * CHUNK, x_eng[i]))
+    for e in range(E):
+        for s in range(PASSES):
+            units.append(("w1", e, s, w1_eng[e][s]))
+            if s == 1 and e > 0 and not (1 and e == LAST):
+                units.append(("w2", e - 1, slice(0, N), w2_eng[e - 1]))
+    if 1:
+        units.append(("w2", LAST - 1, slice(0, N), w2_eng[LAST - 1]))
+    units += [("w2", LAST, slice(0, P), w2_eng[LAST]), ("w2", LAST, slice(P, N), w2_eng[E])]
+    at = {(k, a, b if k == "w1" else (b.start if k == "w2" else b)): u for u, (k, a, b, g) in enumerate(units)}
+    relu_at, qh_at, y_at, sc_at = {}, {}, {}, {}
+    for e in range(E):
+        u = at["w1", e, PASSES - 1]
+        d = (3, 4, 1, 2) if e < LAST - 1 else (1, 4, 3, 5) if e < LAST else (2, 4, 3, 4)
+        relu_at.setdefault(u + d[0], []).append(e)
+        qh_at.setdefault(u + d[1], []).append(e)
+        for cols in ([slice(0, N)] if e < LAST else [slice(0, P), slice(P, N)]):
+            v = max(u + d[1], at["w2", e, cols.start] + 1)
+            y_at.setdefault(v + d[2] - 1, []).append((e, cols))
+            sc_at.setdefault(v + d[3] - 1, []).append((e, cols))
+
+    with ExitStack() as ctx:
+        keep = ctx.enter_context(tc.tile_pool(name="keep", bufs=1))
+        raw_pool = ctx.enter_context(tc.tile_pool(name="raw", bufs=LEAD + 2))
+        raw2_pool = ctx.enter_context(tc.tile_pool(name="raw2", bufs=4))
+        grp_pool = ctx.enter_context(tc.tile_pool(name="grp", bufs=6))
+        code_pool = ctx.enter_context(tc.tile_pool(name="codes", bufs=8))
+        small_pool = ctx.enter_context(tc.tile_pool(name="small", bufs=3))
+        a_psum = ctx.enter_context(tc.psum_pool(name="a_psum", bufs=2))
+        al_psum = ctx.enter_context(tc.psum_pool(name="al_psum", bufs=1))
+        y_psum = ctx.enter_context(tc.psum_pool(name="y_psum", bufs=2))
+
+        offs_sb = keep.tile([P, SLOTS // 16], U16, name="offs_sb")
+        dst_sb = keep.tile([P, SLOTS // 16], U16, name="dst_sb")
+        gate_sb = keep.tile([P, SLOTS], F32, name="gate_sb")
+        x_codes = [keep.tile([P, T], U32, name=f"x_codes{s}", align_bytes=64) for s in range(PASSES)]
+        x_scales = keep.tile([P, T], U8, name="x_scales", align_bytes=64)
+        s_codes = [keep.tile([P, SLOTS], U32, name=f"s_codes{s}", align_bytes=64) for s in range(PASSES)]
+        s_scales = keep.tile([P, SLOTS], U8, name="s_scales", align_bytes=64)
+        out_sb = [keep.tile([P, T], F32, name=f"out_sb{h}") for h in range(N // P)]
+
+        nc.gpsimd.memset(x_scales[:], 0)
+        for h in range(N // P):
+            nc.gpsimd.memset(out_sb[h][:], 0.0)
+
+        raws, grouped, w1q, w2q, hq, hg, abanks, ys = {}, {}, {}, {}, {}, {}, {}, {}
+
+        def load(u):
+            kind, a, b, eng = units[u]
+            if kind == "w2":
+                raw = raw2_pool.tile([P, PACK, b.stop - b.start], F32, name="raw2")
+                src = w2[a, :, b]
+            else:
+                raw = raw_pool.tile([P, PACK, CHUNK], F32, name="raw")
+                if kind == "x":
+                    src = xT[a * PASS : (a + 1) * PASS, b : b + CHUNK]
+                else:
+                    src = w1[a, b * PASS : (b + 1) * PASS, :]
+            nc.sync.dma_start(out=raw[:], in_=src.rearrange("(p j) w -> p j w", j=PACK))
+            raws[u] = raw
+            if u == 0:
+                nc.sync.dma_start(offs_sb[:], offs)
+            if u == 7:
+                nc.sync.dma_start(dst_sb[:], dst)
+                nc.sync.dma_start(out=gate_sb[:], in_=gate[0:P, :])
+
+        def copy(u):
+            kind, a, b, eng = units[u]
+            raw = raws.pop(u)
+            width = b.stop - b.start if kind == "w2" else CHUNK
+            g = grp_pool.tile([P, width * PACK], BF16, name="grp2" if kind == "w2" else "grp", align_bytes=64)
+            for who, lo, hi in eng:
+                lo, hi = lo * width // 16, hi * width // 16
+                if kind == "w1":
+                    src = raw[:, :, lo:hi].rearrange("p j (m t) -> p m j t", t=PACK)
+                    dest = g[:].rearrange("p (t m j) -> p m j t", t=PACK, j=PACK)[:, lo // PACK : hi // PACK]
+                else:
+                    src = raw[:, :, lo:hi].rearrange("p j (c i) -> p c j i", i=4)
+                    dest = g[:, lo * PACK : hi * PACK].rearrange("p (c i j) -> p c j i", i=4, j=PACK)
+                if who == "V":
+                    nc.vector.tensor_copy(out=dest, in_=src)
+                else:
+                    nc.scalar.copy(out=dest, in_=src)
+            grouped[u] = g
+
+        def quantise(u):
+            kind, a, b, eng = units[u]
+            g = grouped.pop(u)
+            if kind == "x":
+                cols = slice(b, b + CHUNK)
+                nc.vector.quantize_mx(
+                    out=x_codes[a][:, cols].bitcast(FP8X4), scales=x_scales[4 * a : P, cols], in_=g[:]
+                )
+                return
+            width = b.stop - b.start if kind == "w2" else CHUNK
+            codes = code_pool.tile([P, width], U32, name="codes" + kind, align_bytes=64)
+            scales = code_pool.tile([P, width], U8, name="scales" + kind, align_bytes=64)
+            nc.vector.quantize_mx(out=codes[:].bitcast(FP8X4), scales=scales[:], in_=g[:])
+            if kind == "w1":
+                w1q[a, b] = (codes, scales)
+            else:
+                w2q[a, b.start] = (codes, scales)
+
+        def gather(to, table, lo, hi):
+            nc.vector.tensor_copy(to[:, lo:hi], table[:].indirect(offs_sb[:, lo // 16 : hi // 16]))
+
+        def matmul1(e, s, t, dest):
+            slots = slice(e * C, (e + 1) * C)
+            codes, scales = w1q[e, s]
+            chans = slice(t * P, (t + 1) * P)
+            nc.tensor.matmul_mx(
+                out=dest,
+                lhsT=codes[:, chans].bitcast(FP8X4),
+                lhsT_scale=scales[:, chans],
+                rhs=s_codes[s][:, slots].bitcast(FP8X4),
+                rhs_scale=s_scales[4 * s : P, slots],
+                start=(s == 0),
+                stop=(s == PASSES - 1),
+            )
+
+        def first_layer(e, s):
+            if e == LAST:
+                if s == 0:
+                    abanks[e] = [al_psum.tile([P, C], F32, name=f"al{t}") for t in range(PACK)]
+                for t in range(PACK):
+                    matmul1(e, s, t, abanks[e][t][:])
+            elif s == PASSES - 1:
+                abanks[e] = a_psum.tile([P, PACK, C], F32, name="a")
+                for t in range(PACK):
+                    for q in range(PASSES):
+                        matmul1(e, q, t, abanks[e][:, t, :])
+
+        def relu2(e):
+            r = small_pool.tile([P, PACK, C], F32, name="r")
+            if e == LAST:
+                for t in range(PACK):
+                    if 'SVSV'[t] == "S":
+                        nc.scalar.activation(r[:, t, :], abanks[e][t][:], RELU)
+                    else:
+                        nc.vector.tensor_scalar_max(r[:, t, :], abanks[e][t][:], 0.0)
+            else:
+                nc.scalar.activation(r[:], abanks[e][:], RELU)
+            g = small_pool.tile([P, C * PACK], BF16, name="hg", align_bytes=64)
+            k = 128 if e == LAST else C
+            rr = r[:, :, 0:k].rearrange("p j c -> p c j")
+            nc.scalar.activation(g[:, 0 : k * PACK].rearrange("p (c j) -> p c j", j=PACK), rr, SQUARE)
+            if k < C:
+                rr = r[:, :, k:C].rearrange("p j c -> p c j")
+                nc.vector.tensor_tensor(g[:, k * PACK :].rearrange("p (c j) -> p c j", j=PACK), rr, rr, MULT)
+            hg[e] = g
+
+        def quantise_h(e):
+            codes = small_pool.tile([P, C], U32, name="hcodes", align_bytes=64)
+            scales = small_pool.tile([P, C], U8, name="hscales", align_bytes=64)
+            nc.vector.quantize_mx(out=codes[:].bitcast(FP8X4), scales=scales[:], in_=hg[e][:])
+            hq[e] = (codes, scales)
+
+        def second_layer(e, cols):
+            y = y_psum.tile([P, cols.stop - cols.start], F32, name="y")
+            codes, scales = w2q[e, cols.start]
+            for i in range((cols.stop - cols.start) // P):
+                chans = slice(i * P, (i + 1) * P)
+                nc.tensor.matmul_mx(
+                    out=y[:, chans],
+                    lhsT=codes[:, chans].bitcast(FP8X4),
+                    lhsT_scale=scales[:, chans],
+                    rhs=hq[e][0][:].bitcast(FP8X4),
+                    rhs_scale=hq[e][1][:],
+                    start=True,
+                    stop=True,
+                )
+            y_sb = small_pool.tile([P, cols.stop - cols.start], F32, name="y_sb")
+            nc.scalar.copy(out=y_sb[:], in_=y[:])
+            ys[e, cols.start] = y_sb
+
+        def scatter(e, cols):
+            for i in range((cols.stop - cols.start) // P):
+                h = cols.start // P + i
+                nc.vector.tensor_tensor(
+                    out_sb[h][:].indirect(dst_sb[:, e * C // 16 : (e + 1) * C // 16]),
+                    ys[e, cols.start][:, i * P : (i + 1) * P],
+                    gate_sb[:, e * C : (e + 1) * C],
+                    MULT,
+                )
+
+        def quantise_and_use(u):
+            kind, a, b, eng = units[u]
+            quantise(u)
+            if kind == "x" and b > 0:
+                if a < PASSES - 1:
+                    gather(s_codes[a], x_codes[a], 0, SLOTS)
+                else:
+                    gather(s_codes[a], x_codes[a], 0, 256)
+                    gather(s_scales, x_scales, 0, 256)
+                    gather(s_codes[a], x_codes[a], 256, SLOTS)
+                    gather(s_scales, x_scales, 256, SLOTS)
+            if kind == "w1":
+                first_layer(a, b)
+
+        for u in range(LEAD):
+            load(u)
+        for step in range(len(units) + 12):
+            if step + LEAD < len(units):
+                load(step + LEAD)
+            if step < len(units):
+                copy(step)
+            if 1 <= step <= len(units):
+                quantise_and_use(step - 1)
+            for e in relu_at.get(step, []):
+                relu2(e)
+            for e in qh_at.get(step, []):
+                quantise_h(e)
+            for e, cols in y_at.get(step, []):
+                second_layer(e, cols)
+            for e, cols in sc_at.get(step, []):
+                scatter(e, cols)
+        for h in range(N // P):
+            nc.sync.dma_start(out=out[h * P : (h + 1) * P, :], in_=out_sb[h][:])

@@ -28,36 +28,13 @@ LAST = E - 1
 def tile_moe_two_mlp_relu2_kernel(tc, xT, w1, w2, gate, offs, dst, out):
     nc = tc.nc
 
-    x_eng = [[('V', 0, 16)], [('V', 0, 16)], [('S', 0, 16)], [('V', 0, 16)], [('S', 0, 16)], [('V', 0, 8), ('S', 8, 16)]]
-    w1_eng = [[[('S', 0, 16)], [('S', 0, 16)], [('S', 0, 16)]], [[('S', 0, 16)], [('V', 0, 16)], [('V', 0, 16)]], [[('S', 0, 16)], [('V', 0, 16)], [('S', 0, 16)]], [[('S', 0, 16)], [('V', 0, 16)], [('S', 0, 16)]], [[('S', 0, 16)], [('V', 0, 16)], [('S', 0, 16)]], [[('S', 0, 16)], [('V', 0, 16)], [('V', 0, 8), ('S', 8, 16)]]]
-    w2_eng = [[('V', 0, 16)], [('V', 0, 16)], [('V', 0, 16)], [('V', 0, 16)], [('V', 0, 16)], [('S', 0, 16)], [('V', 0, 16)]]
-    units = []
-    for i in range(2 * PASSES):
-        units.append(("x", i // 2, i % 2 * CHUNK, x_eng[i]))
-    for e in range(E):
-        for s in range(PASSES):
-            units.append(("w1", e, s, w1_eng[e][s]))
-            if s == 1 and e > 0 and not (1 and e == LAST):
-                units.append(("w2", e - 1, slice(0, N), w2_eng[e - 1]))
-    if 1:
-        units.append(("w2", LAST - 1, slice(0, N), w2_eng[LAST - 1]))
-    units += [("w2", LAST, slice(0, P), w2_eng[LAST]), ("w2", LAST, slice(P, N), w2_eng[E])]
-    at = {(k, a, b if k == "w1" else (b.start if k == "w2" else b)): u for u, (k, a, b, g) in enumerate(units)}
-    relu_at, qh_at, y_at, sc_at = {}, {}, {}, {}
-    for e in range(E):
-        u = at["w1", e, PASSES - 1]
-        d = (3, 4, 1, 2) if e < LAST - 1 else (1, 4, 3, 5) if e < LAST else (2, 4, 3, 4)
-        relu_at.setdefault(u + d[0], []).append(e)
-        qh_at.setdefault(u + d[1], []).append(e)
-        for cols in ([slice(0, N)] if e < LAST else [slice(0, P), slice(P, N)]):
-            v = max(u + d[1], at["w2", e, cols.start] + 1)
-            y_at.setdefault(v + d[2] - 1, []).append((e, cols))
-            sc_at.setdefault(v + d[3] - 1, []).append((e, cols))
+    units = [('x', 0, slice(0, 256, None), [('S', 0, 16)]), ('x', 0, slice(256, 512, None), [('V', 0, 16)]), ('x', 0, slice(512, 1024, None), [('S', 0, 16)]), ('x', 1, slice(0, 512, None), [('V', 0, 16)]), ('x', 1, slice(512, 1024, None), [('S', 0, 16)]), ('x', 2, slice(0, 512, None), [('S', 0, 16)]), ('x', 2, slice(512, 1024, None), [('V', 0, 8), ('S', 8, 16)]), ('w1', 0, 0, [('S', 0, 16)]), ('w1', 0, 1, [('V', 0, 16)]), ('w1', 0, 2, [('S', 0, 16)]), ('w1', 1, 0, [('S', 0, 16)]), ('w2', 0, slice(0, 256, None), [('V', 0, 16)]), ('w1', 1, 1, [('V', 0, 16)]), ('w1', 1, 2, [('S', 0, 16)]), ('w1', 2, 0, [('S', 0, 16)]), ('w2', 1, slice(0, 256, None), [('V', 0, 16)]), ('w1', 2, 1, [('V', 0, 16)]), ('w1', 2, 2, [('S', 0, 16)]), ('w1', 3, 0, [('S', 0, 16)]), ('w2', 2, slice(0, 256, None), [('V', 0, 16)]), ('w1', 3, 1, [('V', 0, 16)]), ('w1', 3, 2, [('S', 0, 16)]), ('w1', 4, 0, [('S', 0, 16)]), ('w2', 3, slice(0, 256, None), [('V', 0, 16)]), ('w1', 4, 1, [('V', 0, 16)]), ('w1', 4, 2, [('S', 0, 16)]), ('w1', 5, 0, [('S', 0, 16)]), ('w1', 5, 1, [('V', 0, 16)]), ('w1', 5, 2, [('S', 0, 8), ('V', 8, 16)]), ('w2', 4, slice(0, 256, None), [('S', 0, 16)]), ('w2', 5, slice(0, 128, None), [('S', 0, 16)]), ('w2', 5, slice(128, 256, None), [('V', 0, 16)])]
 
     with ExitStack() as ctx:
         keep = ctx.enter_context(tc.tile_pool(name="keep", bufs=1))
         raw_pool = ctx.enter_context(tc.tile_pool(name="raw", bufs=LEAD + 2))
         raw2_pool = ctx.enter_context(tc.tile_pool(name="raw2", bufs=4))
+        half_pool = ctx.enter_context(tc.tile_pool(name="half", bufs=2))
         grp_pool = ctx.enter_context(tc.tile_pool(name="grp", bufs=6))
         code_pool = ctx.enter_context(tc.tile_pool(name="codes", bufs=8))
         small_pool = ctx.enter_context(tc.tile_pool(name="small", bufs=3))
@@ -86,28 +63,38 @@ def tile_moe_two_mlp_relu2_kernel(tc, xT, w1, w2, gate, offs, dst, out):
                 raw = raw2_pool.tile([P, PACK, b.stop - b.start], F32, name="raw2")
                 src = w2[a, :, b]
             else:
-                raw = raw_pool.tile([P, PACK, CHUNK], F32, name="raw")
+                if kind == "x" or len(eng) == 1:
+                    raw = raw_pool.tile([P, PACK, b.stop - b.start if kind == "x" else CHUNK], F32, name="raw")
                 if kind == "x":
-                    src = xT[a * PASS : (a + 1) * PASS, b : b + CHUNK]
+                    src = xT[a * PASS : (a + 1) * PASS, b]
                 else:
                     src = w1[a, b * PASS : (b + 1) * PASS, :]
+            if kind == "w1" and len(eng) > 1:
+                raws[u] = []
+                for who, lo, hi in eng:
+                    part = half_pool.tile([P, PACK, (hi - lo) * 32], F32, name="half")
+                    nc.sync.dma_start(
+                        out=part[:], in_=src[:, lo * 32 : hi * 32].rearrange("(p j) w -> p j w", j=PACK)
+                    )
+                    raws[u].append(part)
+                return
             nc.sync.dma_start(out=raw[:], in_=src.rearrange("(p j) w -> p j w", j=PACK))
             raws[u] = raw
             if u == 0:
                 nc.sync.dma_start(offs_sb[:], offs)
-            if u == 7:
+            if u == 12:
                 nc.sync.dma_start(dst_sb[:], dst)
                 nc.sync.dma_start(out=gate_sb[:], in_=gate[0:P, :])
 
         def copy(u):
             kind, a, b, eng = units[u]
             raw = raws.pop(u)
-            width = b.stop - b.start if kind == "w2" else CHUNK
+            width = b.stop - b.start if kind != "w1" else CHUNK
             g = grp_pool.tile([P, width * PACK], BF16, name="grp2" if kind == "w2" else "grp", align_bytes=64)
             for who, lo, hi in eng:
                 lo, hi = lo * width // 16, hi * width // 16
                 if kind == "w1":
-                    src = raw[:, :, lo:hi].rearrange("p j (m t) -> p m j t", t=PACK)
+                    src = (raw.pop(0)[:] if len(eng) > 1 else raw[:]).rearrange("p j (m t) -> p m j t", t=PACK)
                     dest = g[:].rearrange("p (t m j) -> p m j t", t=PACK, j=PACK)[:, lo // PACK : hi // PACK]
                 else:
                     src = raw[:, :, lo:hi].rearrange("p j (c i) -> p c j i", i=4)
@@ -122,7 +109,7 @@ def tile_moe_two_mlp_relu2_kernel(tc, xT, w1, w2, gate, offs, dst, out):
             kind, a, b, eng = units[u]
             g = grouped.pop(u)
             if kind == "x":
-                cols = slice(b, b + CHUNK)
+                cols = b
                 nc.vector.quantize_mx(
                     out=x_codes[a][:, cols].bitcast(FP8X4), scales=x_scales[4 * a : P, cols], in_=g[:]
                 )
@@ -190,7 +177,8 @@ def tile_moe_two_mlp_relu2_kernel(tc, xT, w1, w2, gate, offs, dst, out):
             nc.vector.quantize_mx(out=codes[:].bitcast(FP8X4), scales=scales[:], in_=hg[e][:])
             hq[e] = (codes, scales)
 
-        def second_layer(e, cols):
+        def second_layer(e, i):
+            cols = slice(0, N) if i is None else slice(i * P, (i + 1) * P)
             y = y_psum.tile([P, cols.stop - cols.start], F32, name="y")
             codes, scales = w2q[e, cols.start]
             for i in range((cols.stop - cols.start) // P):
@@ -208,12 +196,11 @@ def tile_moe_two_mlp_relu2_kernel(tc, xT, w1, w2, gate, offs, dst, out):
             nc.scalar.copy(out=y_sb[:], in_=y[:])
             ys[e, cols.start] = y_sb
 
-        def scatter(e, cols):
-            for i in range((cols.stop - cols.start) // P):
-                h = cols.start // P + i
+        def scatter(e, h):
+            for key, i in ([((e, 0), h)] if e < LAST else [((e, h * P), 0)]):
                 nc.vector.tensor_tensor(
                     out_sb[h][:].indirect(dst_sb[:, e * C // 16 : (e + 1) * C // 16]),
-                    ys[e, cols.start][:, i * P : (i + 1) * P],
+                    ys[key][:, i * P : (i + 1) * P],
                     gate_sb[:, e * C : (e + 1) * C],
                     MULT,
                 )
@@ -221,7 +208,7 @@ def tile_moe_two_mlp_relu2_kernel(tc, xT, w1, w2, gate, offs, dst, out):
         def quantise_and_use(u):
             kind, a, b, eng = units[u]
             quantise(u)
-            if kind == "x" and b > 0:
+            if kind == "x" and b.stop == T:
                 if a < PASSES - 1:
                     gather(s_codes[a], x_codes[a], 0, SLOTS)
                 else:
@@ -232,22 +219,7 @@ def tile_moe_two_mlp_relu2_kernel(tc, xT, w1, w2, gate, offs, dst, out):
             if kind == "w1":
                 first_layer(a, b)
 
-        for u in range(LEAD):
-            load(u)
-        for step in range(len(units) + 12):
-            if step + LEAD < len(units):
-                load(step + LEAD)
-            if step < len(units):
-                copy(step)
-            if 1 <= step <= len(units):
-                quantise_and_use(step - 1)
-            for e in relu_at.get(step, []):
-                relu2(e)
-            for e in qh_at.get(step, []):
-                quantise_h(e)
-            for e, cols in y_at.get(step, []):
-                second_layer(e, cols)
-            for e, cols in sc_at.get(step, []):
-                scatter(e, cols)
+        for name, *args in [('load', 0), ('load', 1), ('load', 2), ('load', 3), ('load', 4), ('load', 5), ('load', 6), ('load', 7), ('load', 8), ('load', 9), ('copy', 0), ('load', 10), ('copy', 1), ('q', 0), ('load', 11), ('copy', 2), ('q', 1), ('load', 12), ('copy', 3), ('q', 2), ('load', 13), ('copy', 4), ('q', 3), ('load', 14), ('copy', 5), ('q', 4), ('load', 15), ('copy', 6), ('q', 5), ('load', 16), ('copy', 7), ('q', 6), ('load', 17), ('copy', 8), ('q', 7), ('load', 18), ('copy', 9), ('q', 8), ('load', 19), ('copy', 10), ('q', 9), ('load', 20), ('copy', 11), ('q', 10), ('relu', 0), ('load', 21), ('copy', 12), ('q', 11), ('qh', 0), ('load', 22), ('copy', 13), ('q', 12), ('y', 0, None), ('load', 23), ('copy', 14), ('q', 13), ('sc', 0, 0), ('sc', 0, 1), ('load', 24), ('copy', 15), ('q', 14), ('relu', 1), ('load', 25), ('copy', 16), ('q', 15), ('qh', 1), ('load', 26), ('copy', 17), ('q', 16), ('y', 1, None), ('load', 27), ('copy', 18), ('q', 17), ('sc', 1, 0), ('sc', 1, 1), ('load', 28), ('copy', 19), ('q', 18), ('relu', 2), ('load', 29), ('copy', 20), ('q', 19), ('qh', 2), ('load', 30), ('copy', 21), ('q', 20), ('y', 2, None), ('load', 31), ('copy', 22), ('q', 21), ('sc', 2, 0), ('sc', 2, 1), ('copy', 23), ('q', 22), ('relu', 3), ('copy', 24), ('q', 23), ('qh', 3), ('copy', 25), ('q', 24), ('y', 3, None), ('copy', 26), ('q', 25), ('relu', 4), ('sc', 3, 0), ('sc', 3, 1), ('copy', 27), ('q', 26), ('qh', 4), ('copy', 28), ('q', 27), ('copy', 29), ('q', 28), ('copy', 30), ('q', 29), ('relu', 5), ('copy', 31), ('q', 30), ('qh', 5), ('y', 4, None), ('y', 5, 0), ('q', 31), ('y', 5, 1), ('sc', 4, 0), ('sc', 4, 1), ('sc', 5, 0), ('sc', 5, 1)]:
+            {"load": load, "copy": copy, "q": quantise_and_use, "relu": relu2, "qh": quantise_h, "y": second_layer, "sc": scatter}[name](*args)
         for h in range(N // P):
             nc.sync.dma_start(out=out[h * P : (h + 1) * P, :], in_=out_sb[h][:])

@@ -19,28 +19,27 @@ P = 128
 PACK = 4
 PASS = P * PACK
 PASSES = K // PASS
-CHUNK = 512
 SLOTS = E * C
-LEAD = 9
+HALVES = N // P
 LAST = E - 1
+LEAD = 8
 
 
 def tile_moe_two_mlp_relu2_kernel(tc, xT, w1, w2, gate, offs, dst, out):
     nc = tc.nc
-
-    units = [('x', 0, slice(0, 256, None), [('S', 0, 16)]), ('x', 0, slice(256, 512, None), [('V', 0, 16)]), ('x', 0, slice(512, 1024, None), [('S', 0, 16)]), ('x', 1, slice(0, 512, None), [('V', 0, 16)]), ('x', 1, slice(512, 1024, None), [('S', 0, 16)]), ('x', 2, slice(0, 512, None), [('S', 0, 16)]), ('x', 2, slice(512, 1024, None), [('V', 0, 8), ('S', 8, 16)]), ('w1', 0, 0, [('S', 0, 16)]), ('w1', 0, 1, [('V', 0, 16)]), ('w1', 0, 2, [('S', 0, 16)]), ('w1', 1, 0, [('S', 0, 16)]), ('w2', 0, slice(0, 256, None), [('V', 0, 16)]), ('w1', 1, 1, [('V', 0, 16)]), ('w1', 1, 2, [('S', 0, 16)]), ('w1', 2, 0, [('S', 0, 16)]), ('w2', 1, slice(0, 256, None), [('V', 0, 16)]), ('w1', 2, 1, [('V', 0, 16)]), ('w1', 2, 2, [('S', 0, 16)]), ('w1', 3, 0, [('S', 0, 16)]), ('w2', 2, slice(0, 256, None), [('V', 0, 16)]), ('w1', 3, 1, [('V', 0, 16)]), ('w1', 3, 2, [('S', 0, 16)]), ('w1', 4, 0, [('S', 0, 16)]), ('w2', 3, slice(0, 256, None), [('V', 0, 16)]), ('w1', 4, 1, [('V', 0, 16)]), ('w1', 4, 2, [('S', 0, 16)]), ('w1', 5, 0, [('S', 0, 16)]), ('w1', 5, 1, [('V', 0, 16)]), ('w1', 5, 2, [('S', 0, 8), ('V', 8, 16)]), ('w2', 4, slice(0, 256, None), [('S', 0, 16)]), ('w2', 5, slice(0, 128, None), [('S', 0, 16)]), ('w2', 5, slice(128, 256, None), [('V', 0, 16)])]
+    units = [('x', 0, 0, [('S', 0, 256)]), ('x', 0, 0, [('V', 256, 512)]), ('x', 0, 0, [('S', 512, 1024)]), ('x', 0, 1, [('V', 0, 512)]), ('x', 0, 1, [('S', 512, 1024)]), ('x', 0, 2, [('S', 0, 512)]), ('x', 0, 2, [('V', 512, 768), ('S', 768, 1024)]), ('w1', 0, 0, [('S', 0, 512)]), ('w1', 0, 1, [('V', 0, 512)]), ('w1', 0, 2, [('S', 0, 512)]), ('w1', 1, 0, [('S', 0, 512)]), ('w2', 0, 0, [('S', 0, 256)]), ('w1', 1, 1, [('V', 0, 512)]), ('w1', 1, 2, [('S', 0, 512)]), ('w1', 2, 0, [('S', 0, 512)]), ('w2', 1, 0, [('V', 0, 256)]), ('w1', 2, 1, [('V', 0, 512)]), ('w1', 2, 2, [('S', 0, 512)]), ('w1', 3, 0, [('S', 0, 512)]), ('w2', 2, 0, [('S', 0, 256)]), ('w1', 3, 1, [('V', 0, 512)]), ('w1', 3, 2, [('S', 0, 512)]), ('w1', 4, 0, [('S', 0, 512)]), ('w2', 3, 0, [('V', 0, 256)]), ('w1', 4, 1, [('V', 0, 512)]), ('w1', 4, 2, [('S', 0, 512)]), ('w1', 5, 0, [('S', 0, 512)]), ('w1', 5, 1, [('V', 0, 512)]), ('w1', 5, 2, [('S', 0, 256), ('V', 256, 512)]), ('w2', 4, 0, [('S', 0, 256)]), ('w2', 5, 0, [('S', 0, 256)])]
+    relu_delay, h_delay, y_delay, scatter_delay = (2, 3, 2, 3)
 
     with ExitStack() as ctx:
         keep = ctx.enter_context(tc.tile_pool(name="keep", bufs=1))
-        raw_pool = ctx.enter_context(tc.tile_pool(name="raw", bufs=LEAD + 2))
-        raw2_pool = ctx.enter_context(tc.tile_pool(name="raw2", bufs=4))
-        half_pool = ctx.enter_context(tc.tile_pool(name="half", bufs=2))
-        grp_pool = ctx.enter_context(tc.tile_pool(name="grp", bufs=6))
+        raw_pool = ctx.enter_context(tc.tile_pool(name="raw", bufs=12))
+        raw2_pool = ctx.enter_context(tc.tile_pool(name="raw2", bufs=3))
+        grouped_pool = ctx.enter_context(tc.tile_pool(name="grouped", bufs=6))
         code_pool = ctx.enter_context(tc.tile_pool(name="codes", bufs=8))
         small_pool = ctx.enter_context(tc.tile_pool(name="small", bufs=3))
         a_psum = ctx.enter_context(tc.psum_pool(name="a_psum", bufs=2))
-        al_psum = ctx.enter_context(tc.psum_pool(name="al_psum", bufs=1))
-        y_psum = ctx.enter_context(tc.psum_pool(name="y_psum", bufs=2))
+        last_psum = ctx.enter_context(tc.psum_pool(name="last_psum", bufs=1))
+        y_psum = ctx.enter_context(tc.psum_pool(name="y_psum", bufs=1))
 
         offs_sb = keep.tile([P, SLOTS // 16], U16, name="offs_sb")
         dst_sb = keep.tile([P, SLOTS // 16], U16, name="dst_sb")
@@ -49,37 +48,28 @@ def tile_moe_two_mlp_relu2_kernel(tc, xT, w1, w2, gate, offs, dst, out):
         x_scales = keep.tile([P, T], U8, name="x_scales", align_bytes=64)
         s_codes = [keep.tile([P, SLOTS], U32, name=f"s_codes{s}", align_bytes=64) for s in range(PASSES)]
         s_scales = keep.tile([P, SLOTS], U8, name="s_scales", align_bytes=64)
-        out_sb = [keep.tile([P, T], F32, name=f"out_sb{h}") for h in range(N // P)]
+        out_sb = [keep.tile([P, T], F32, name=f"out_sb{h}") for h in range(HALVES)]
 
         nc.gpsimd.memset(x_scales[:], 0)
-        for h in range(N // P):
+        for h in range(HALVES):
             nc.gpsimd.memset(out_sb[h][:], 0.0)
 
-        raws, grouped, w1q, w2q, hq, hg, abanks, ys = {}, {}, {}, {}, {}, {}, {}, {}
+        raws, grouped, quantised, hidden, sums, results = {}, {}, {}, {}, {}, {}
 
         def load(u):
-            kind, a, b, eng = units[u]
-            if kind == "w2":
-                raw = raw2_pool.tile([P, PACK, b.stop - b.start], F32, name="raw2")
-                src = w2[a, :, b]
-            else:
-                if kind == "x" or len(eng) == 1:
-                    raw = raw_pool.tile([P, PACK, b.stop - b.start if kind == "x" else CHUNK], F32, name="raw")
+            kind, a, s, pieces = units[u]
+            raws[u] = []
+            for eng, c0, c1 in pieces:
+                pool = raw2_pool if kind == "w2" else raw_pool
+                raw = pool.tile([P, PACK, c1 - c0], F32, name="raw")
                 if kind == "x":
-                    src = xT[a * PASS : (a + 1) * PASS, b]
+                    src = xT[s * PASS : (s + 1) * PASS, c0:c1]
+                elif kind == "w1":
+                    src = w1[a, s * PASS : (s + 1) * PASS, c0:c1]
                 else:
-                    src = w1[a, b * PASS : (b + 1) * PASS, :]
-            if kind == "w1" and len(eng) > 1:
-                raws[u] = []
-                for who, lo, hi in eng:
-                    part = half_pool.tile([P, PACK, (hi - lo) * 32], F32, name="half")
-                    nc.sync.dma_start(
-                        out=part[:], in_=src[:, lo * 32 : hi * 32].rearrange("(p j) w -> p j w", j=PACK)
-                    )
-                    raws[u].append(part)
-                return
-            nc.sync.dma_start(out=raw[:], in_=src.rearrange("(p j) w -> p j w", j=PACK))
-            raws[u] = raw
+                    src = w2[a, :, c0:c1]
+                nc.sync.dma_start(out=raw[:], in_=src.rearrange("(p j) c -> p j c", j=PACK))
+                raws[u].append(raw)
             if u == 0:
                 nc.sync.dma_start(offs_sb[:], offs)
             if u == 12:
@@ -87,51 +77,65 @@ def tile_moe_two_mlp_relu2_kernel(tc, xT, w1, w2, gate, offs, dst, out):
                 nc.sync.dma_start(out=gate_sb[:], in_=gate[0:P, :])
 
         def copy(u):
-            kind, a, b, eng = units[u]
-            raw = raws.pop(u)
-            width = b.stop - b.start if kind != "w1" else CHUNK
-            g = grp_pool.tile([P, width * PACK], BF16, name="grp2" if kind == "w2" else "grp", align_bytes=64)
-            for who, lo, hi in eng:
-                lo, hi = lo * width // 16, hi * width // 16
+            kind, a, s, pieces = units[u]
+            first, end = pieces[0][1], pieces[-1][2]
+            g = grouped_pool.tile(
+                [P, (end - first) * PACK], BF16, name="grouped2" if kind == "w2" else "grouped", align_bytes=64
+            )
+            for (eng, c0, c1), raw in zip(pieces, raws.pop(u)):
                 if kind == "w1":
-                    src = (raw.pop(0)[:] if len(eng) > 1 else raw[:]).rearrange("p j (m t) -> p m j t", t=PACK)
-                    dest = g[:].rearrange("p (t m j) -> p m j t", t=PACK, j=PACK)[:, lo // PACK : hi // PACK]
+                    src = raw[:].rearrange("p j (m t) -> p m j t", t=PACK)
+                    dest = g[:].rearrange("p (t m j) -> p m j t", t=PACK, j=PACK)[:, c0 // PACK : c1 // PACK]
                 else:
-                    src = raw[:, :, lo:hi].rearrange("p j (c i) -> p c j i", i=4)
-                    dest = g[:, lo * PACK : hi * PACK].rearrange("p (c i j) -> p c j i", i=4, j=PACK)
-                if who == "V":
+                    src = raw[:].rearrange("p j (c i) -> p c j i", i=4)
+                    dest = g[:, (c0 - first) * PACK : (c1 - first) * PACK].rearrange(
+                        "p (c i j) -> p c j i", i=4, j=PACK
+                    )
+                if eng == "V":
                     nc.vector.tensor_copy(out=dest, in_=src)
                 else:
                     nc.scalar.copy(out=dest, in_=src)
             grouped[u] = g
 
         def quantise(u):
-            kind, a, b, eng = units[u]
+            kind, a, s, pieces = units[u]
             g = grouped.pop(u)
+            first, end = pieces[0][1], pieces[-1][2]
             if kind == "x":
-                cols = b
-                nc.vector.quantize_mx(
-                    out=x_codes[a][:, cols].bitcast(FP8X4), scales=x_scales[4 * a : P, cols], in_=g[:]
-                )
-                return
-            width = b.stop - b.start if kind == "w2" else CHUNK
-            codes = code_pool.tile([P, width], U32, name="codes" + kind, align_bytes=64)
-            scales = code_pool.tile([P, width], U8, name="scales" + kind, align_bytes=64)
-            nc.vector.quantize_mx(out=codes[:].bitcast(FP8X4), scales=scales[:], in_=g[:])
-            if kind == "w1":
-                w1q[a, b] = (codes, scales)
+                codes, scales = x_codes[s][:, first:end], x_scales[4 * s : P, first:end]
             else:
-                w2q[a, b.start] = (codes, scales)
+                codes = code_pool.tile([P, end - first], U32, name="codes" + kind, align_bytes=64)[:, :]
+                scales = code_pool.tile([P, end - first], U8, name="scales" + kind, align_bytes=64)[:, :]
+                quantised[kind, a, s] = (codes, scales)
+            nc.vector.quantize_mx(out=codes.bitcast(FP8X4), scales=scales, in_=g[:])
+            if kind == "x" and end == T:
+                cuts = [(0, SLOTS)] if s < PASSES - 1 else [(0, 2 * C), (2 * C, SLOTS)]
+                for lo, hi in cuts:
+                    gather(s_codes[s], x_codes[s], lo, hi)
+                    if s == PASSES - 1:
+                        gather(s_scales, x_scales, lo, hi)
+            if kind == "w1":
+                if a == LAST:
+                    if s == 0:
+                        sums[a] = [last_psum.tile([P, C], F32, name=f"last{t}")[:, :] for t in range(PACK)]
+                    for t in range(PACK):
+                        first_layer(a, t, s)
+                elif s == PASSES - 1:
+                    bank = a_psum.tile([P, PACK, C], F32, name="bank")
+                    sums[a] = [bank[:, t, :] for t in range(PACK)] + [bank[:, :, :]]
+                    for t in range(PACK):
+                        for q in range(PASSES):
+                            first_layer(a, t, q)
 
         def gather(to, table, lo, hi):
             nc.vector.tensor_copy(to[:, lo:hi], table[:].indirect(offs_sb[:, lo // 16 : hi // 16]))
 
-        def matmul1(e, s, t, dest):
+        def first_layer(e, t, s):
             slots = slice(e * C, (e + 1) * C)
-            codes, scales = w1q[e, s]
+            codes, scales = quantised["w1", e, s]
             chans = slice(t * P, (t + 1) * P)
             nc.tensor.matmul_mx(
-                out=dest,
+                out=sums[e][t],
                 lhsT=codes[:, chans].bitcast(FP8X4),
                 lhsT_scale=scales[:, chans],
                 rhs=s_codes[s][:, slots].bitcast(FP8X4),
@@ -140,86 +144,80 @@ def tile_moe_two_mlp_relu2_kernel(tc, xT, w1, w2, gate, offs, dst, out):
                 stop=(s == PASSES - 1),
             )
 
-        def first_layer(e, s):
-            if e == LAST:
-                if s == 0:
-                    abanks[e] = [al_psum.tile([P, C], F32, name=f"al{t}") for t in range(PACK)]
-                for t in range(PACK):
-                    matmul1(e, s, t, abanks[e][t][:])
-            elif s == PASSES - 1:
-                abanks[e] = a_psum.tile([P, PACK, C], F32, name="a")
-                for t in range(PACK):
-                    for q in range(PASSES):
-                        matmul1(e, q, t, abanks[e][:, t, :])
-
         def relu2(e):
             r = small_pool.tile([P, PACK, C], F32, name="r")
+            g = small_pool.tile([P, C * PACK], BF16, name="h", align_bytes=64)
+            split = 64 if e == LAST else C
             if e == LAST:
                 for t in range(PACK):
                     if 'SVSV'[t] == "S":
-                        nc.scalar.activation(r[:, t, :], abanks[e][t][:], RELU)
+                        nc.scalar.activation(r[:, t, :], sums[e][t], RELU)
                     else:
-                        nc.vector.tensor_scalar_max(r[:, t, :], abanks[e][t][:], 0.0)
+                        nc.vector.tensor_scalar_max(r[:, t, :], sums[e][t], 0.0)
             else:
-                nc.scalar.activation(r[:], abanks[e][:], RELU)
-            g = small_pool.tile([P, C * PACK], BF16, name="hg", align_bytes=64)
-            k = 128 if e == LAST else C
-            rr = r[:, :, 0:k].rearrange("p j c -> p c j")
-            nc.scalar.activation(g[:, 0 : k * PACK].rearrange("p (c j) -> p c j", j=PACK), rr, SQUARE)
-            if k < C:
-                rr = r[:, :, k:C].rearrange("p j c -> p c j")
-                nc.vector.tensor_tensor(g[:, k * PACK :].rearrange("p (c j) -> p c j", j=PACK), rr, rr, MULT)
-            hg[e] = g
+                nc.scalar.activation(r[:], sums[e][PACK], RELU)
+            src = r[:, :, 0:split].rearrange("p j c -> p c j")
+            nc.scalar.activation(g[:, 0 : split * PACK].rearrange("p (c j) -> p c j", j=PACK), src, SQUARE)
+            if split < C:
+                src = r[:, :, split:C].rearrange("p j c -> p c j")
+                nc.vector.tensor_tensor(g[:, split * PACK :].rearrange("p (c j) -> p c j", j=PACK), src, src, MULT)
+            hidden[e] = g
 
         def quantise_h(e):
-            codes = small_pool.tile([P, C], U32, name="hcodes", align_bytes=64)
-            scales = small_pool.tile([P, C], U8, name="hscales", align_bytes=64)
-            nc.vector.quantize_mx(out=codes[:].bitcast(FP8X4), scales=scales[:], in_=hg[e][:])
-            hq[e] = (codes, scales)
+            codes = small_pool.tile([P, C], U32, name="h_codes", align_bytes=64)
+            scales = small_pool.tile([P, C], U8, name="h_scales", align_bytes=64)
+            nc.vector.quantize_mx(out=codes[:].bitcast(FP8X4), scales=scales[:], in_=hidden[e][:])
+            hidden[e] = (codes, scales)
 
-        def second_layer(e, i):
-            cols = slice(0, N) if i is None else slice(i * P, (i + 1) * P)
-            y = y_psum.tile([P, cols.stop - cols.start], F32, name="y")
-            codes, scales = w2q[e, cols.start]
-            for i in range((cols.stop - cols.start) // P):
-                chans = slice(i * P, (i + 1) * P)
-                nc.tensor.matmul_mx(
-                    out=y[:, chans],
-                    lhsT=codes[:, chans].bitcast(FP8X4),
-                    lhsT_scale=scales[:, chans],
-                    rhs=hq[e][0][:].bitcast(FP8X4),
-                    rhs_scale=hq[e][1][:],
-                    start=True,
-                    stop=True,
-                )
-            y_sb = small_pool.tile([P, cols.stop - cols.start], F32, name="y_sb")
-            nc.scalar.copy(out=y_sb[:], in_=y[:])
-            ys[e, cols.start] = y_sb
+        def second_layer(e):
+            ys = [[0], [1]] if e == LAST else [range(HALVES)]
+            for halves in ys:
+                y = y_psum.tile([P, len(halves), C], F32, name=f"y{halves[0]}")
+                codes, scales = quantised["w2", e, 0]
+                for i, h in enumerate(halves):
+                    chans = slice(h * P, (h + 1) * P)
+                    nc.tensor.matmul_mx(
+                        out=y[:, i, :],
+                        lhsT=codes[:, chans].bitcast(FP8X4),
+                        lhsT_scale=scales[:, chans],
+                        rhs=hidden[e][0][:].bitcast(FP8X4),
+                        rhs_scale=hidden[e][1][:],
+                        start=True,
+                        stop=True,
+                    )
+                y_sb = small_pool.tile([P, len(halves), C], F32, name=f"y_sb{halves[0]}")
+                nc.scalar.copy(out=y_sb[:], in_=y[:])
+                for i, h in enumerate(halves):
+                    results[e, h] = y_sb[:, i, :]
 
-        def scatter(e, h):
-            for key, i in ([((e, 0), h)] if e < LAST else [((e, h * P), 0)]):
+        def scatter(e):
+            for h in range(HALVES):
                 nc.vector.tensor_tensor(
                     out_sb[h][:].indirect(dst_sb[:, e * C // 16 : (e + 1) * C // 16]),
-                    ys[key][:, i * P : (i + 1) * P],
+                    results[e, h],
                     gate_sb[:, e * C : (e + 1) * C],
                     MULT,
                 )
+                if e == LAST:
+                    nc.sync.dma_start(out=out[h * P : (h + 1) * P, :], in_=out_sb[h][:])
 
-        def quantise_and_use(u):
-            kind, a, b, eng = units[u]
-            quantise(u)
-            if kind == "x" and b.stop == T:
-                if a < PASSES - 1:
-                    gather(s_codes[a], x_codes[a], 0, SLOTS)
-                else:
-                    gather(s_codes[a], x_codes[a], 0, 256)
-                    gather(s_scales, x_scales, 0, 256)
-                    gather(s_codes[a], x_codes[a], 256, SLOTS)
-                    gather(s_scales, x_scales, 256, SLOTS)
-            if kind == "w1":
-                first_layer(a, b)
-
-        for name, *args in [('load', 0), ('load', 1), ('load', 2), ('load', 3), ('load', 4), ('load', 5), ('load', 6), ('load', 7), ('load', 8), ('load', 9), ('copy', 0), ('load', 10), ('copy', 1), ('q', 0), ('load', 11), ('copy', 2), ('q', 1), ('load', 12), ('copy', 3), ('q', 2), ('load', 13), ('copy', 4), ('q', 3), ('load', 14), ('copy', 5), ('q', 4), ('load', 15), ('copy', 6), ('q', 5), ('load', 16), ('copy', 7), ('q', 6), ('load', 17), ('copy', 8), ('q', 7), ('load', 18), ('copy', 9), ('q', 8), ('load', 19), ('copy', 10), ('q', 9), ('load', 20), ('copy', 11), ('q', 10), ('relu', 0), ('load', 21), ('copy', 12), ('q', 11), ('qh', 0), ('load', 22), ('copy', 13), ('q', 12), ('y', 0, None), ('load', 23), ('copy', 14), ('q', 13), ('sc', 0, 0), ('sc', 0, 1), ('load', 24), ('copy', 15), ('q', 14), ('relu', 1), ('load', 25), ('copy', 16), ('q', 15), ('qh', 1), ('load', 26), ('copy', 17), ('q', 16), ('y', 1, None), ('load', 27), ('copy', 18), ('q', 17), ('sc', 1, 0), ('sc', 1, 1), ('load', 28), ('copy', 19), ('q', 18), ('relu', 2), ('load', 29), ('copy', 20), ('q', 19), ('qh', 2), ('load', 30), ('copy', 21), ('q', 20), ('y', 2, None), ('load', 31), ('copy', 22), ('q', 21), ('sc', 2, 0), ('sc', 2, 1), ('copy', 23), ('q', 22), ('relu', 3), ('copy', 24), ('q', 23), ('qh', 3), ('copy', 25), ('q', 24), ('y', 3, None), ('copy', 26), ('q', 25), ('relu', 4), ('sc', 3, 0), ('sc', 3, 1), ('copy', 27), ('q', 26), ('qh', 4), ('copy', 28), ('q', 27), ('copy', 29), ('q', 28), ('copy', 30), ('q', 29), ('relu', 5), ('copy', 31), ('q', 30), ('qh', 5), ('y', 4, None), ('y', 5, 0), ('q', 31), ('y', 5, 1), ('sc', 4, 0), ('sc', 4, 1), ('sc', 5, 0), ('sc', 5, 1)]:
-            {"load": load, "copy": copy, "q": quantise_and_use, "relu": relu2, "qh": quantise_h, "y": second_layer, "sc": scatter}[name](*args)
-        for h in range(N // P):
-            nc.sync.dma_start(out=out[h * P : (h + 1) * P, :], in_=out_sb[h][:])
+        todo = {}
+        for u in range(LEAD):
+            load(u)
+        for step in range(len(units) + 8):
+            if step + LEAD < len(units):
+                load(step + LEAD)
+            if step < len(units):
+                copy(step)
+            if 1 <= step <= len(units):
+                kind, a, s, pieces = units[step - 1]
+                quantise(step - 1)
+                if kind == "w1" and s == PASSES - 1:
+                    todo.setdefault(step - 1 + relu_delay, []).append((relu2, a))
+                    todo.setdefault(step - 1 + h_delay, []).append((quantise_h, a))
+                if kind == "w2":
+                    ready = max(step, [i for i, v in enumerate(units) if v[:3] == ("w1", a, PASSES - 1)][0] + h_delay)
+                    todo.setdefault(ready + y_delay - 1, []).append((second_layer, a))
+                    todo.setdefault(ready + scatter_delay - 1, []).append((scatter, a))
+            for action, e in todo.pop(step, []):
+                action(e)

@@ -22,202 +22,219 @@ PASSES = K // PASS
 SLOTS = E * C
 HALVES = N // P
 LAST = E - 1
-LEAD = 8
+WIDTH = 512
+AHEAD = 8
+LIST_ROWS = 16
+
+X_COPIERS = ("SV", "S", "V", "S", "S", "VS")
+W1_COPIERS = ("S", "V", "S")
+W1_LAST_COPIERS = ("S", "V", "SV")
+W2_COPIERS = ("V", "V", "V", "V", "S", "S")
 
 
 def tile_moe_two_mlp_relu2_kernel(tc, xT, w1, w2, gate, offs, dst, out):
     nc = tc.nc
-    units = [('x', 0, 0, [('S', 0, 256)]), ('x', 0, 0, [('V', 256, 512)]), ('x', 0, 0, [('S', 512, 1024)]), ('x', 0, 1, [('V', 0, 512)]), ('x', 0, 1, [('S', 512, 1024)]), ('x', 0, 2, [('S', 0, 512)]), ('x', 0, 2, [('V', 512, 768), ('S', 768, 1024)]), ('w1', 0, 0, [('S', 0, 512)]), ('w1', 0, 1, [('V', 0, 512)]), ('w1', 0, 2, [('S', 0, 512)]), ('w1', 1, 0, [('S', 0, 512)]), ('w2', 0, 0, [('S', 0, 256)]), ('w1', 1, 1, [('V', 0, 512)]), ('w1', 1, 2, [('S', 0, 512)]), ('w1', 2, 0, [('S', 0, 512)]), ('w2', 1, 0, [('V', 0, 256)]), ('w1', 2, 1, [('V', 0, 512)]), ('w1', 2, 2, [('S', 0, 512)]), ('w1', 3, 0, [('S', 0, 512)]), ('w2', 2, 0, [('S', 0, 256)]), ('w1', 3, 1, [('V', 0, 512)]), ('w1', 3, 2, [('S', 0, 512)]), ('w1', 4, 0, [('S', 0, 512)]), ('w2', 3, 0, [('V', 0, 256)]), ('w1', 4, 1, [('V', 0, 512)]), ('w1', 4, 2, [('S', 0, 512)]), ('w1', 5, 0, [('S', 0, 512)]), ('w1', 5, 1, [('V', 0, 512)]), ('w1', 5, 2, [('S', 0, 256), ('V', 256, 512)]), ('w2', 4, 0, [('S', 0, 256)]), ('w2', 5, 0, [('S', 0, 256)])]
-    relu_delay, h_delay, y_delay, scatter_delay = (2, 3, 2, 3)
+
+    jobs = []
+    for i, copiers in enumerate(X_COPIERS):
+        jobs.append(("x", 0, i * WIDTH // T, i * WIDTH % T, WIDTH, copiers))
+    for e in range(E):
+        for s in range(PASSES):
+            copiers = W1_LAST_COPIERS[s] if e == LAST else W1_COPIERS[s]
+            jobs.append(("w1", e, s, 0, H, copiers))
+            if s == 0 and 0 < e < LAST:
+                jobs.append(("w2", e - 1, 0, 0, N, W2_COPIERS[e - 1]))
+    for e in (LAST - 1, LAST):
+        jobs.append(("w2", e, 0, 0, N, W2_COPIERS[e]))
 
     with ExitStack() as ctx:
         keep = ctx.enter_context(tc.tile_pool(name="keep", bufs=1))
-        raw_pool = ctx.enter_context(tc.tile_pool(name="raw", bufs=12))
+        raw_pool = ctx.enter_context(tc.tile_pool(name="raw", bufs=AHEAD + 4))
         raw2_pool = ctx.enter_context(tc.tile_pool(name="raw2", bufs=3))
         grouped_pool = ctx.enter_context(tc.tile_pool(name="grouped", bufs=6))
         code_pool = ctx.enter_context(tc.tile_pool(name="codes", bufs=8))
         small_pool = ctx.enter_context(tc.tile_pool(name="small", bufs=3))
-        a_psum = ctx.enter_context(tc.psum_pool(name="a_psum", bufs=2))
+        sum_psum = ctx.enter_context(tc.psum_pool(name="sum_psum", bufs=2))
         last_psum = ctx.enter_context(tc.psum_pool(name="last_psum", bufs=1))
         y_psum = ctx.enter_context(tc.psum_pool(name="y_psum", bufs=1))
 
-        offs_sb = keep.tile([P, SLOTS // 16], U16, name="offs_sb")
-        dst_sb = keep.tile([P, SLOTS // 16], U16, name="dst_sb")
+        offs_sb = keep.tile([P, SLOTS // LIST_ROWS], U16, name="offs_sb")
+        dst_sb = keep.tile([P, SLOTS // LIST_ROWS], U16, name="dst_sb")
         gate_sb = keep.tile([P, SLOTS], F32, name="gate_sb")
         x_codes = [keep.tile([P, T], U32, name=f"x_codes{s}", align_bytes=64) for s in range(PASSES)]
         x_scales = keep.tile([P, T], U8, name="x_scales", align_bytes=64)
-        s_codes = [keep.tile([P, SLOTS], U32, name=f"s_codes{s}", align_bytes=64) for s in range(PASSES)]
-        s_scales = keep.tile([P, SLOTS], U8, name="s_scales", align_bytes=64)
-        out_sb = [keep.tile([P, T], F32, name=f"out_sb{h}") for h in range(HALVES)]
+        slot_codes = [keep.tile([P, SLOTS], U32, name=f"slot_codes{s}", align_bytes=64) for s in range(PASSES)]
+        slot_scales = keep.tile([P, SLOTS], U8, name="slot_scales", align_bytes=64)
+        out_sb = [keep.tile([P, T], F32, name=f"out_sb{half}") for half in range(HALVES)]
 
         nc.gpsimd.memset(x_scales[:], 0)
-        for h in range(HALVES):
-            nc.gpsimd.memset(out_sb[h][:], 0.0)
+        for half in range(HALVES):
+            nc.gpsimd.memset(out_sb[half][:], 0.0)
 
-        raws, grouped, quantised, hidden, sums, results = {}, {}, {}, {}, {}, {}
+        raws, grouped, weights, hidden, sums, results = {}, {}, {}, {}, {}, {}
 
-        def load(u):
-            kind, a, s, pieces = units[u]
-            raws[u] = []
-            for eng, c0, c1 in pieces:
-                pool = raw2_pool if kind == "w2" else raw_pool
-                raw = pool.tile([P, PACK, c1 - c0], F32, name="raw")
-                if kind == "x":
-                    src = xT[s * PASS : (s + 1) * PASS, c0:c1]
-                elif kind == "w1":
-                    src = w1[a, s * PASS : (s + 1) * PASS, c0:c1]
+        def load(i):
+            tensor, e, s, first, width, copiers = jobs[i]
+            part = width // len(copiers)
+            raws[i] = []
+            for c0 in range(first, first + width, part):
+                if tensor == "x":
+                    raw = raw_pool.tile([P, PACK, part], F32, name="raw")
+                    src = xT[s * PASS : (s + 1) * PASS, c0 : c0 + part]
+                elif tensor == "w1":
+                    raw = raw_pool.tile([P, PACK, part], F32, name="raw")
+                    src = w1[e, s * PASS : (s + 1) * PASS, c0 : c0 + part]
                 else:
-                    src = w2[a, :, c0:c1]
+                    raw = raw2_pool.tile([P, PACK, part], F32, name="raw2")
+                    src = w2[e, :, c0 : c0 + part]
                 nc.sync.dma_start(out=raw[:], in_=src.rearrange("(p j) c -> p j c", j=PACK))
-                raws[u].append(raw)
-            if u == 0:
+                raws[i].append(raw)
+            if i == 0:
                 nc.sync.dma_start(offs_sb[:], offs)
-            if u == 12:
+            if i == AHEAD + 3:
                 nc.sync.dma_start(dst_sb[:], dst)
                 nc.sync.dma_start(out=gate_sb[:], in_=gate[0:P, :])
 
-        def copy(u):
-            kind, a, s, pieces = units[u]
-            first, end = pieces[0][1], pieces[-1][2]
-            g = grouped_pool.tile(
-                [P, (end - first) * PACK], BF16, name="grouped2" if kind == "w2" else "grouped", align_bytes=64
+        def copy(i):
+            tensor, e, s, first, width, copiers = jobs[i]
+            part = width // len(copiers)
+            tile = grouped_pool.tile(
+                [P, width * PACK], BF16, name="grouped2" if tensor == "w2" else "grouped", align_bytes=64
             )
-            for (eng, c0, c1), raw in zip(pieces, raws.pop(u)):
-                if kind == "w1":
+            for n, (copier, raw) in enumerate(zip(copiers, raws.pop(i))):
+                if tensor == "w1":
                     src = raw[:].rearrange("p j (m t) -> p m j t", t=PACK)
-                    dest = g[:].rearrange("p (t m j) -> p m j t", t=PACK, j=PACK)[:, c0 // PACK : c1 // PACK]
+                    dest = tile[:].rearrange("p (t m j) -> p m j t", t=PACK, j=PACK)
+                    dest = dest[:, n * part // PACK : (n + 1) * part // PACK]
                 else:
                     src = raw[:].rearrange("p j (c i) -> p c j i", i=4)
-                    dest = g[:, (c0 - first) * PACK : (c1 - first) * PACK].rearrange(
-                        "p (c i j) -> p c j i", i=4, j=PACK
-                    )
-                if eng == "V":
-                    nc.vector.tensor_copy(out=dest, in_=src)
-                else:
+                    dest = tile[:, n * part * PACK : (n + 1) * part * PACK]
+                    dest = dest.rearrange("p (c i j) -> p c j i", i=4, j=PACK)
+                if copier == "S":
                     nc.scalar.copy(out=dest, in_=src)
-            grouped[u] = g
+                else:
+                    nc.vector.tensor_copy(out=dest, in_=src)
+            grouped[i] = tile
 
-        def quantise(u):
-            kind, a, s, pieces = units[u]
-            g = grouped.pop(u)
-            first, end = pieces[0][1], pieces[-1][2]
-            if kind == "x":
-                codes, scales = x_codes[s][:, first:end], x_scales[4 * s : P, first:end]
+        def quantise(i):
+            tensor, e, s, first, width, copiers = jobs[i]
+            if tensor == "x":
+                codes = x_codes[s][:, first : first + width]
+                scales = x_scales[4 * s : P, first : first + width]
             else:
-                codes = code_pool.tile([P, end - first], U32, name="codes" + kind, align_bytes=64)[:, :]
-                scales = code_pool.tile([P, end - first], U8, name="scales" + kind, align_bytes=64)[:, :]
-                quantised[kind, a, s] = (codes, scales)
-            nc.vector.quantize_mx(out=codes.bitcast(FP8X4), scales=scales, in_=g[:])
-            if kind == "x" and end == T:
-                cuts = [(0, SLOTS)] if s < PASSES - 1 else [(0, 2 * C), (2 * C, SLOTS)]
-                for lo, hi in cuts:
-                    gather(s_codes[s], x_codes[s], lo, hi)
-                    if s == PASSES - 1:
-                        gather(s_scales, x_scales, lo, hi)
-            if kind == "w1":
-                if a == LAST:
-                    if s == 0:
-                        sums[a] = [last_psum.tile([P, C], F32, name=f"last{t}")[:, :] for t in range(PACK)]
-                    for t in range(PACK):
-                        first_layer(a, t, s)
-                elif s == PASSES - 1:
-                    bank = a_psum.tile([P, PACK, C], F32, name="bank")
-                    sums[a] = [bank[:, t, :] for t in range(PACK)] + [bank[:, :, :]]
-                    for t in range(PACK):
-                        for q in range(PASSES):
-                            first_layer(a, t, q)
+                codes = code_pool.tile([P, width], U32, name="codes_" + tensor, align_bytes=64)[:, :]
+                scales = code_pool.tile([P, width], U8, name="scales_" + tensor, align_bytes=64)[:, :]
+                weights[tensor, e, s] = (codes, scales)
+            nc.vector.quantize_mx(out=codes.bitcast(FP8X4), scales=scales, in_=grouped.pop(i)[:])
 
-        def gather(to, table, lo, hi):
-            nc.vector.tensor_copy(to[:, lo:hi], table[:].indirect(offs_sb[:, lo // 16 : hi // 16]))
+        def gather(slots, table, first, end):
+            listed = offs_sb[:, first // LIST_ROWS : end // LIST_ROWS]
+            nc.vector.tensor_copy(slots[:, first:end], table[:].indirect(listed))
 
-        def first_layer(e, t, s):
+        def gather_pass(s):
+            if s < PASSES - 1:
+                gather(slot_codes[s], x_codes[s], 0, SLOTS)
+                return
+            for first, end in ((0, 2 * C), (2 * C, SLOTS)):
+                gather(slot_codes[s], x_codes[s], first, end)
+                gather(slot_scales, x_scales, first, end)
+
+        def first_layer(e, group, s, into):
+            codes, scales = weights["w1", e, s]
+            chans = slice(group * P, (group + 1) * P)
             slots = slice(e * C, (e + 1) * C)
-            codes, scales = quantised["w1", e, s]
-            chans = slice(t * P, (t + 1) * P)
             nc.tensor.matmul_mx(
-                out=sums[e][t],
+                out=into,
                 lhsT=codes[:, chans].bitcast(FP8X4),
                 lhsT_scale=scales[:, chans],
-                rhs=s_codes[s][:, slots].bitcast(FP8X4),
-                rhs_scale=s_scales[4 * s : P, slots],
+                rhs=slot_codes[s][:, slots].bitcast(FP8X4),
+                rhs_scale=slot_scales[4 * s : P, slots],
                 start=(s == 0),
                 stop=(s == PASSES - 1),
             )
 
-        def relu2(e):
-            r = small_pool.tile([P, PACK, C], F32, name="r")
-            g = small_pool.tile([P, C * PACK], BF16, name="h", align_bytes=64)
-            split = 64 if e == LAST else C
-            if e == LAST:
-                for t in range(PACK):
-                    if 'SVSV'[t] == "S":
-                        nc.scalar.activation(r[:, t, :], sums[e][t], RELU)
-                    else:
-                        nc.vector.tensor_scalar_max(r[:, t, :], sums[e][t], 0.0)
-            else:
-                nc.scalar.activation(r[:], sums[e][PACK], RELU)
-            src = r[:, :, 0:split].rearrange("p j c -> p c j")
-            nc.scalar.activation(g[:, 0 : split * PACK].rearrange("p (c j) -> p c j", j=PACK), src, SQUARE)
-            if split < C:
-                src = r[:, :, split:C].rearrange("p j c -> p c j")
-                nc.vector.tensor_tensor(g[:, split * PACK :].rearrange("p (c j) -> p c j", j=PACK), src, src, MULT)
-            hidden[e] = g
+        def first_layer_and_relu(e):
+            bank = sum_psum.tile([P, PACK, C], F32, name="bank")
+            for group in range(PACK):
+                for s in range(PASSES):
+                    first_layer(e, group, s, bank[:, group, :])
+            relu = small_pool.tile([P, PACK, C], F32, name="relu")
+            nc.scalar.activation(relu[:], bank[:], RELU)
+            return relu
 
-        def quantise_h(e):
+        def last_first_layer(s):
+            if s == 0:
+                for group in range(PACK):
+                    sums[group] = last_psum.tile([P, C], F32, name=f"last{group}")
+            for group in range(PACK):
+                first_layer(LAST, group, s, sums[group][:])
+
+        def last_relu():
+            relu = small_pool.tile([P, PACK, C], F32, name="relu")
+            for group in range(PACK):
+                if group % 2 == 0:
+                    nc.scalar.activation(relu[:, group, :], sums[group][:], RELU)
+                else:
+                    nc.vector.tensor_scalar_max(relu[:, group, :], sums[group][:], 0.0)
+            return relu
+
+        def square_and_quantise(e, relu):
+            tile = small_pool.tile([P, C * PACK], BF16, name="h", align_bytes=64)
+            h = tile[:].rearrange("p (c t) -> p c t", t=PACK)
+            r = relu[:].rearrange("p t c -> p c t")
+            if e < LAST:
+                nc.scalar.activation(h, r, SQUARE)
+            else:
+                nc.scalar.activation(h[:, 0 : C // 2], r[:, 0 : C // 2], SQUARE)
+                nc.vector.tensor_tensor(h[:, C // 2 :], r[:, C // 2 :], r[:, C // 2 :], MULT)
             codes = small_pool.tile([P, C], U32, name="h_codes", align_bytes=64)
             scales = small_pool.tile([P, C], U8, name="h_scales", align_bytes=64)
-            nc.vector.quantize_mx(out=codes[:].bitcast(FP8X4), scales=scales[:], in_=hidden[e][:])
+            nc.vector.quantize_mx(out=codes[:].bitcast(FP8X4), scales=scales[:], in_=tile[:])
             hidden[e] = (codes, scales)
 
         def second_layer(e):
-            ys = [[0], [1]] if e == LAST else [range(HALVES)]
-            for halves in ys:
-                y = y_psum.tile([P, len(halves), C], F32, name=f"y{halves[0]}")
-                codes, scales = quantised["w2", e, 0]
-                for i, h in enumerate(halves):
-                    chans = slice(h * P, (h + 1) * P)
+            w_codes, w_scales = weights["w2", e, 0]
+            h_codes, h_scales = hidden[e]
+            for members in [range(HALVES)] if e < LAST else [[half] for half in range(HALVES)]:
+                y = y_psum.tile([P, len(members), C], F32, name=f"y{members[0]}")
+                for n, half in enumerate(members):
+                    chans = slice(half * P, (half + 1) * P)
                     nc.tensor.matmul_mx(
-                        out=y[:, i, :],
-                        lhsT=codes[:, chans].bitcast(FP8X4),
-                        lhsT_scale=scales[:, chans],
-                        rhs=hidden[e][0][:].bitcast(FP8X4),
-                        rhs_scale=hidden[e][1][:],
+                        out=y[:, n, :],
+                        lhsT=w_codes[:, chans].bitcast(FP8X4),
+                        lhsT_scale=w_scales[:, chans],
+                        rhs=h_codes[:].bitcast(FP8X4),
+                        rhs_scale=h_scales[:],
                         start=True,
                         stop=True,
                     )
-                y_sb = small_pool.tile([P, len(halves), C], F32, name=f"y_sb{halves[0]}")
+                y_sb = small_pool.tile([P, len(members), C], F32, name=f"y_sb{members[0]}")
                 nc.scalar.copy(out=y_sb[:], in_=y[:])
-                for i, h in enumerate(halves):
-                    results[e, h] = y_sb[:, i, :]
+                for n, half in enumerate(members):
+                    results[e, half] = y_sb[:, n, :]
 
         def scatter(e):
-            for h in range(HALVES):
+            listed = dst_sb[:, e * C // LIST_ROWS : (e + 1) * C // LIST_ROWS]
+            for half in range(HALVES):
                 nc.vector.tensor_tensor(
-                    out_sb[h][:].indirect(dst_sb[:, e * C // 16 : (e + 1) * C // 16]),
-                    results[e, h],
-                    gate_sb[:, e * C : (e + 1) * C],
-                    MULT,
+                    out_sb[half][:].indirect(listed), results[e, half], gate_sb[:, e * C : (e + 1) * C], MULT
                 )
                 if e == LAST:
-                    nc.sync.dma_start(out=out[h * P : (h + 1) * P, :], in_=out_sb[h][:])
+                    nc.sync.dma_start(out=out[half * P : (half + 1) * P, :], in_=out_sb[half][:])
 
-        todo = {}
-        for u in range(LEAD):
-            load(u)
-        for step in range(len(units) + 8):
-            if step + LEAD < len(units):
-                load(step + LEAD)
-            if step < len(units):
-                copy(step)
-            if 1 <= step <= len(units):
-                kind, a, s, pieces = units[step - 1]
-                quantise(step - 1)
-                if kind == "w1" and s == PASSES - 1:
-                    todo.setdefault(step - 1 + relu_delay, []).append((relu2, a))
-                    todo.setdefault(step - 1 + h_delay, []).append((quantise_h, a))
-                if kind == "w2":
-                    ready = max(step, [i for i, v in enumerate(units) if v[:3] == ("w1", a, PASSES - 1)][0] + h_delay)
-                    todo.setdefault(ready + y_delay - 1, []).append((second_layer, a))
-                    todo.setdefault(ready + scatter_delay - 1, []).append((scatter, a))
-            for action, e in todo.pop(step, []):
-                action(e)
+        for i in range(AHEAD):
+            load(i)
+        for i, (tensor, e, s, first, width, copiers) in enumerate(jobs):
+            if i + AHEAD < len(jobs):
+                load(i + AHEAD)
+            copy(i)
+            quantise(i)
+            if tensor == "x" and first + width == T:
+                gather_pass(s)
+            if tensor == "w1" and e == LAST:
+                last_first_layer(s)
+            if tensor == "w1" and s == PASSES - 1:
+                square_and_quantise(e, last_relu() if e == LAST else first_layer_and_relu(e))
+            if tensor == "w2":
+                second_layer(e)
+                scatter(e)

from contextlib import ExitStack

import concourse.mybir as mybir

K, T, E, C, H, N = 1536, 1024, 6, 128, 512, 256
FLOPS = 2 * E * C * (K * H + H * N)

F32 = mybir.dt.float32
BF16 = mybir.dt.bfloat16
U32 = mybir.dt.uint32
U16 = mybir.dt.uint16
U8 = mybir.dt.uint8
FP8X4 = mybir.dt.float8_e4m3fn_x4
RELU = mybir.ActivationFunctionType.Relu
SQUARE = mybir.ActivationFunctionType.Square
MULT = mybir.AluOpType.mult

P = 128
PACK = 4
PASS = P * PACK
PASSES = K // PASS
SLOTS = E * C
HALVES = N // P
LAST = E - 1
WIDTH = 512
AHEAD = 8
LIST_ROWS = 16

X_COPIERS = ("SV", "S", "V", "S", "S", "VS")
W1_COPIERS = ("S", "V", "S")
W1_LAST_COPIERS = ("S", "V", "SV")
W2_COPIERS = ("V", "V", "V", "V", "S", "S")


def tile_moe_two_mlp_relu2_kernel(tc, xT, w1, w2, gate, offs, dst, out):
    nc = tc.nc

    jobs = []
    for i, copiers in enumerate(X_COPIERS):
        jobs.append(("x", 0, i * WIDTH // T, i * WIDTH % T, WIDTH, copiers))
    for e in range(E):
        for s in range(PASSES):
            copiers = W1_LAST_COPIERS[s] if e == LAST else W1_COPIERS[s]
            jobs.append(("w1", e, s, 0, H, copiers))
            if s == 0 and 0 < e < LAST:
                jobs.append(("w2", e - 1, 0, 0, N, W2_COPIERS[e - 1]))
    for e in (LAST - 1, LAST):
        jobs.append(("w2", e, 0, 0, N, W2_COPIERS[e]))

    with ExitStack() as ctx:
        keep = ctx.enter_context(tc.tile_pool(name="keep", bufs=1))
        raw_pool = ctx.enter_context(tc.tile_pool(name="raw", bufs=AHEAD + 4))
        raw2_pool = ctx.enter_context(tc.tile_pool(name="raw2", bufs=3))
        grouped_pool = ctx.enter_context(tc.tile_pool(name="grouped", bufs=6))
        code_pool = ctx.enter_context(tc.tile_pool(name="codes", bufs=8))
        small_pool = ctx.enter_context(tc.tile_pool(name="small", bufs=3))
        sum_psum = ctx.enter_context(tc.psum_pool(name="sum_psum", bufs=2))
        last_psum = ctx.enter_context(tc.psum_pool(name="last_psum", bufs=1))
        y_psum = ctx.enter_context(tc.psum_pool(name="y_psum", bufs=1))

        offs_sb = keep.tile([P, SLOTS // LIST_ROWS], U16, name="offs_sb")
        dst_sb = keep.tile([P, SLOTS // LIST_ROWS], U16, name="dst_sb")
        gate_sb = keep.tile([P, SLOTS], F32, name="gate_sb")
        x_codes = [keep.tile([P, T], U32, name=f"x_codes{s}", align_bytes=64) for s in range(PASSES)]
        x_scales = keep.tile([P, T], U8, name="x_scales", align_bytes=64)
        slot_codes = [keep.tile([P, SLOTS], U32, name=f"slot_codes{s}", align_bytes=64) for s in range(PASSES)]
        slot_scales = keep.tile([P, SLOTS], U8, name="slot_scales", align_bytes=64)
        out_sb = [keep.tile([P, T], F32, name=f"out_sb{half}") for half in range(HALVES)]

        nc.gpsimd.memset(x_scales[:], 0)
        for half in range(HALVES):
            nc.gpsimd.memset(out_sb[half][:], 0.0)

        raws, grouped, weights, hidden, sums, results = {}, {}, {}, {}, {}, {}

        def load(i):
            tensor, e, s, first, width, copiers = jobs[i]
            part = width // len(copiers)
            raws[i] = []
            for c0 in range(first, first + width, part):
                if tensor == "x":
                    raw = raw_pool.tile([P, PACK, part], F32, name="raw")
                    src = xT[s * PASS : (s + 1) * PASS, c0 : c0 + part]
                elif tensor == "w1":
                    raw = raw_pool.tile([P, PACK, part], F32, name="raw")
                    src = w1[e, s * PASS : (s + 1) * PASS, c0 : c0 + part]
                else:
                    raw = raw2_pool.tile([P, PACK, part], F32, name="raw2")
                    src = w2[e, :, c0 : c0 + part]
                nc.sync.dma_start(out=raw[:], in_=src.rearrange("(p j) c -> p j c", j=PACK))
                raws[i].append(raw)
            if i == 0:
                nc.sync.dma_start(offs_sb[:], offs)
            if i == AHEAD + 3:
                nc.sync.dma_start(dst_sb[:], dst)
                nc.sync.dma_start(out=gate_sb[:], in_=gate[0:P, :])

        def copy(i):
            tensor, e, s, first, width, copiers = jobs[i]
            part = width // len(copiers)
            tile = grouped_pool.tile(
                [P, width * PACK], BF16, name="grouped2" if tensor == "w2" else "grouped", align_bytes=64
            )
            for n, (copier, raw) in enumerate(zip(copiers, raws.pop(i))):
                if tensor == "w1":
                    src = raw[:].rearrange("p j (m t) -> p m j t", t=PACK)
                    dest = tile[:].rearrange("p (t m j) -> p m j t", t=PACK, j=PACK)
                    dest = dest[:, n * part // PACK : (n + 1) * part // PACK]
                else:
                    src = raw[:].rearrange("p j (c i) -> p c j i", i=4)
                    dest = tile[:, n * part * PACK : (n + 1) * part * PACK]
                    dest = dest.rearrange("p (c i j) -> p c j i", i=4, j=PACK)
                if copier == "S":
                    nc.scalar.copy(out=dest, in_=src)
                else:
                    nc.vector.tensor_copy(out=dest, in_=src)
            grouped[i] = tile

        def quantise(i):
            tensor, e, s, first, width, copiers = jobs[i]
            if tensor == "x":
                codes = x_codes[s][:, first : first + width]
                scales = x_scales[4 * s : P, first : first + width]
            else:
                codes = code_pool.tile([P, width], U32, name="codes_" + tensor, align_bytes=64)[:, :]
                scales = code_pool.tile([P, width], U8, name="scales_" + tensor, align_bytes=64)[:, :]
                weights[tensor, e, s] = (codes, scales)
            nc.vector.quantize_mx(out=codes.bitcast(FP8X4), scales=scales, in_=grouped.pop(i)[:])

        def gather(slots, table, first, end):
            listed = offs_sb[:, first // LIST_ROWS : end // LIST_ROWS]
            nc.vector.tensor_copy(slots[:, first:end], table[:].indirect(listed))

        def gather_pass(s):
            if s < PASSES - 1:
                gather(slot_codes[s], x_codes[s], 0, SLOTS)
                return
            for first, end in ((0, 2 * C), (2 * C, SLOTS)):
                gather(slot_codes[s], x_codes[s], first, end)
                gather(slot_scales, x_scales, first, end)

        def first_layer(e, group, s, into):
            codes, scales = weights["w1", e, s]
            chans = slice(group * P, (group + 1) * P)
            slots = slice(e * C, (e + 1) * C)
            nc.tensor.matmul_mx(
                out=into,
                lhsT=codes[:, chans].bitcast(FP8X4),
                lhsT_scale=scales[:, chans],
                rhs=slot_codes[s][:, slots].bitcast(FP8X4),
                rhs_scale=slot_scales[4 * s : P, slots],
                start=(s == 0),
                stop=(s == PASSES - 1),
            )

        def first_layer_and_relu(e):
            bank = sum_psum.tile([P, PACK, C], F32, name="bank")
            for group in range(PACK):
                for s in range(PASSES):
                    first_layer(e, group, s, bank[:, group, :])
            relu = small_pool.tile([P, PACK, C], F32, name="relu")
            nc.scalar.activation(relu[:], bank[:], RELU)
            return relu

        def last_first_layer(s):
            if s == 0:
                for group in range(PACK):
                    sums[group] = last_psum.tile([P, C], F32, name=f"last{group}")
            for group in range(PACK):
                first_layer(LAST, group, s, sums[group][:])

        def last_relu():
            relu = small_pool.tile([P, PACK, C], F32, name="relu")
            for group in range(PACK):
                if group % 2 == 0:
                    nc.scalar.activation(relu[:, group, :], sums[group][:], RELU)
                else:
                    nc.vector.tensor_scalar_max(relu[:, group, :], sums[group][:], 0.0)
            return relu

        def square_and_quantise(e, relu):
            tile = small_pool.tile([P, C * PACK], BF16, name="h", align_bytes=64)
            h = tile[:].rearrange("p (c t) -> p c t", t=PACK)
            r = relu[:].rearrange("p t c -> p c t")
            if e < LAST:
                nc.scalar.activation(h, r, SQUARE)
            else:
                nc.scalar.activation(h[:, 0 : C // 2], r[:, 0 : C // 2], SQUARE)
                nc.vector.tensor_tensor(h[:, C // 2 :], r[:, C // 2 :], r[:, C // 2 :], MULT)
            codes = small_pool.tile([P, C], U32, name="h_codes", align_bytes=64)
            scales = small_pool.tile([P, C], U8, name="h_scales", align_bytes=64)
            nc.vector.quantize_mx(out=codes[:].bitcast(FP8X4), scales=scales[:], in_=tile[:])
            hidden[e] = (codes, scales)

        def second_layer(e):
            w_codes, w_scales = weights["w2", e, 0]
            h_codes, h_scales = hidden[e]
            for members in [range(HALVES)] if e < LAST else [[half] for half in range(HALVES)]:
                y = y_psum.tile([P, len(members), C], F32, name=f"y{members[0]}")
                for n, half in enumerate(members):
                    chans = slice(half * P, (half + 1) * P)
                    nc.tensor.matmul_mx(
                        out=y[:, n, :],
                        lhsT=w_codes[:, chans].bitcast(FP8X4),
                        lhsT_scale=w_scales[:, chans],
                        rhs=h_codes[:].bitcast(FP8X4),
                        rhs_scale=h_scales[:],
                        start=True,
                        stop=True,
                    )
                y_sb = small_pool.tile([P, len(members), C], F32, name=f"y_sb{members[0]}")
                nc.scalar.copy(out=y_sb[:], in_=y[:])
                for n, half in enumerate(members):
                    results[e, half] = y_sb[:, n, :]

        def scatter(e):
            listed = dst_sb[:, e * C // LIST_ROWS : (e + 1) * C // LIST_ROWS]
            for half in range(HALVES):
                nc.vector.tensor_tensor(
                    out_sb[half][:].indirect(listed), results[e, half], gate_sb[:, e * C : (e + 1) * C], MULT
                )
                if e == LAST:
                    nc.sync.dma_start(out=out[half * P : (half + 1) * P, :], in_=out_sb[half][:])

        for i in range(AHEAD):
            load(i)
        for i, (tensor, e, s, first, width, copiers) in enumerate(jobs):
            if i + AHEAD < len(jobs):
                load(i + AHEAD)
            copy(i)
            quantise(i)
            if tensor == "x" and first + width == T:
                gather_pass(s)
            if tensor == "w1" and e == LAST:
                last_first_layer(s)
            if tensor == "w1" and s == PASSES - 1:
                square_and_quantise(e, last_relu() if e == LAST else first_layer_and_relu(e))
            if tensor == "w2":
                second_layer(e)
                scatter(e)
